import numpy as np
import ml_dtypes


def mxq(x, axis, fmt="e4m3"):
    dtype, down = {"e4m3": (ml_dtypes.float8_e4m3fn, 7), "e5m2": (ml_dtypes.float8_e5m2, 14)}[fmt]
    v = np.moveaxis(np.asarray(x, np.float32).astype(ml_dtypes.bfloat16).astype(np.float64), axis, -1)
    blocks = v.reshape(v.shape[:-1] + (-1, 32))
    amax = np.abs(blocks).max(-1, keepdims=True)
    byte = np.maximum(np.where(amax > 0, np.frexp(amax)[1] - 1 + 127, 0) - down, 1)
    scale = np.exp2(byte - 127.0)
    codes = (blocks / scale).astype(np.float32).astype(dtype).astype(np.float64)
    return np.moveaxis((codes * scale).reshape(v.shape), -1, axis)


WIDE = False


def mx_kscale(k):
    if not WIDE:
        return np.ones(k)
    levels = np.array([10, -10, 5, -5, 0])
    if k % 512:
        return np.exp2(np.random.permutation(np.resize(levels, k // 32))).repeat(32)
    a = np.empty((k // 512, 16))
    for p in range(k // 512):
        a[p, :8] = np.random.permutation(np.resize(levels, 8))
        for g in range(8):
            far = levels[np.abs(levels - a[p, g]) >= 10]
            a[p, g + 8] = far[np.random.randint(len(far))]
    return np.exp2(a.ravel()).repeat(32)


BF16 = ml_dtypes.bfloat16


def bf(x):
    return np.asarray(x, np.float32).astype(BF16)


def f64(x):
    return np.asarray(x).astype(np.float64)


E2M1 = np.array([0.0, 0.5, 1.0, 1.5, 2.0, 3.0, 4.0, 6.0, -0.0, -0.5, -1.0, -1.5, -2.0, -3.0, -4.0, -6.0])


def pack_weight(w, fmt):
    k, n = w.shape
    w = f64(bf(w)).reshape(k // 32, 32, n)
    amax = np.abs(w).max(1)
    if fmt == "e4m3":
        byte = np.frexp(amax)[1] - 1 + 127 - 7
    else:
        mant, ex = np.frexp(amax / 6.0)
        byte = np.where(mant > 0.5, ex, ex - 1) + 127
    byte = np.clip(np.where(amax > 0, byte, 1), 1, 254)
    scaled = (w * np.exp2(127.0 - byte)[:, None, :]).reshape(k, n).astype(np.float32)
    by_word = np.ascontiguousarray(scaled.reshape(k // 512, 128, 4, n).transpose(0, 1, 3, 2))
    if fmt == "e4m3":
        words = by_word.astype(ml_dtypes.float8_e4m3fn).view(np.uint8)
    else:
        c = by_word.astype(ml_dtypes.float4_e2m1fn).view(np.uint8) & 0xF
        words = c[..., 0::2] | (c[..., 1::2] << 4)
    return np.ascontiguousarray(words), np.ascontiguousarray(byte.astype(np.uint8).reshape(k // 512, 16, n))


def unpack_weight(words, scales, fmt):
    g, p, n, _ = words.shape
    if fmt == "e4m3":
        vals = np.ascontiguousarray(words).view(ml_dtypes.float8_e4m3fn).astype(np.float64)
    else:
        nib = np.empty((g, p, n, 4), np.uint8)
        nib[..., 0::2] = words & 0xF
        nib[..., 1::2] = words >> 4
        vals = E2M1[nib]
    vals = vals * np.repeat(np.exp2(scales.astype(np.float64) - 127.0), 8, axis=1)[..., None]
    return vals.transpose(0, 1, 3, 2).reshape(g * 512, n)
def pack4(w):
    words, scales = pack_weight(w, "e2m1")
    return words.reshape(words.shape[0], 128, -1), scales


def unpack4(words, scales):
    return unpack_weight(words.reshape(words.shape[0], 128, -1, 2), scales, "e2m1")


M, K, F, N = 1024, 2048, 1024, 1024


def setup_inputs():
    s = mx_kscale(K)
    t = mx_kscale(F)
    x = np.random.standard_normal((K, M)) * s[:, None]
    w = np.random.standard_normal((K, F)) / np.sqrt(K) / s[:, None] * t
    b = 0.4 * np.random.standard_normal(F) * t
    c = 2.0 * np.random.standard_normal((F, N)) / np.sqrt(F) / t[:, None]
    v = 2.0 * np.random.standard_normal((F, N)) / np.sqrt(F) / t[:, None]
    x_words, x_scales = pack4(x)
    w_words, w_scales = pack4(w)
    c_words, c_scales = pack_weight(c, "e4m3")
    return {"x_words": x_words, "x_scales": x_scales,
            "w_words": w_words, "w_scales": w_scales,
            "b": bf(b),
            "c_words": c_words, "c_scales": c_scales,
            "v": bf(v)}


def reference(x_words, x_scales, w_words, w_scales, b, c_words, c_scales, v):
    x = unpack4(x_words, x_scales)
    w = unpack4(w_words, w_scales)
    h = np.maximum((x.T @ w) + f64(b), 0.0)
    hq = mxq(h, 1, "e4m3")
    click = hq @ unpack_weight(c_words, c_scales, "e4m3")
    conv = hq @ mxq(f64(v), 0, "e4m3")
    p_click = 1.0 / (1.0 + np.exp(-click))
    p_conv = 1.0 / (1.0 + np.exp(-conv))
    return p_click, p_click * p_conv

@@ -1,0 +1,272 @@
+from contextlib import ExitStack
+
+import concourse.mybir as mybir
+
+M, K, F, N = 1024, 2048, 1024, 1024
+FLOPS = 2 * M * K * F + 2 * 2 * M * F * N
+
+F32 = mybir.dt.float32
+BF16 = mybir.dt.bfloat16
+I32 = mybir.dt.int32
+U32 = mybir.dt.uint32
+U8 = mybir.dt.uint8
+FP8X4 = mybir.dt.float8_e4m3fn_x4
+FP4X4 = mybir.dt.float4_e2m1fn_x4
+ACT = mybir.ActivationFunctionType
+
+P = 128
+PACK = 4
+KG = K // 512
+FG = F // 512
+HALF = 512
+USERS = 128
+
+
+def tile_entire_space_conversion_s4_kernel(
+    tc, x_words, x_scales, w_words, w_scales, b, c_words, c_scales, v, out_0, out_1
+):
+    nc = tc.nc
+    with ExitStack() as ctx:
+        keep = ctx.enter_context(tc.tile_pool(name="keep", bufs=1))
+        stage = ctx.enter_context(tc.tile_pool(name="stage", bufs=3))
+        outs = ctx.enter_context(tc.tile_pool(name="outs", bufs=4))
+        psum = ctx.enter_context(tc.psum_pool(name="psum", bufs=8))
+        ctx.enter_context(tc.manual_schedule())
+
+        w_raw = keep.tile([P, KG, 2 * F], U8, align_bytes=64, name="w_raw")
+        w_codes = keep.tile([P, KG, FG, PACK, 2 * P], U8, align_bytes=64, name="w_codes")
+        w_sraw = keep.tile([P, KG, F], U8, align_bytes=64, name="w_sraw")
+        w_sc = keep.tile([P, KG, FG, PACK, P], U8, align_bytes=64, name="w_sc")
+        x_codes = keep.tile([P, KG, 2 * M], U8, align_bytes=64, name="x_codes")
+        x_sc = keep.tile([P, KG, M], U8, align_bytes=64, name="x_sc")
+        c_codes = keep.tile([P, FG, 4 * N], U8, align_bytes=64, name="c_codes")
+        c_sc = keep.tile([P, FG, N], U8, align_bytes=64, name="c_sc")
+        v_raw = [keep.tile([P, PACK, N], BF16, align_bytes=64, name="v_raw%d" % g) for g in range(FG)]
+        v_pack = [
+            [keep.tile([P, HALF, PACK], BF16, align_bytes=64, name="v_pack%d%d" % (g, n)) for n in range(2)]
+            for g in range(FG)
+        ]
+        v_codes = keep.tile([P, FG, N], U32, align_bytes=64, name="v_codes")
+        v_sc = keep.tile([P, FG, N], U8, align_bytes=64, name="v_sc")
+        h_codes = keep.tile([P, 2, FG, HALF], U32, align_bytes=64, name="h_codes")
+        h_sc = keep.tile([P, 2, FG, HALF], U8, align_bytes=64, name="h_sc")
+        b_col = keep.tile([P, FG, PACK], BF16, align_bytes=64, name="b_col")
+        warm = keep.tile([P, 1], F32, name="warm")
+
+        nc.vector.memset(warm[:], 0.0)
+        nc.scalar.activation(out=warm[:], in_=warm[:], func=ACT.Sigmoid)
+        nc.vector.memset(w_sraw[:].rearrange("p g n -> p (g n)").bitcast(I32), 0)
+        nc.gpsimd.memset(x_sc[:].rearrange("p g n -> p (g n)").bitcast(I32), 0)
+        nc.gpsimd.memset(c_sc[:].rearrange("p g n -> p (g n)").bitcast(I32), 0)
+        nc.gpsimd.dma_start(out=b_col[:], in_=b.rearrange("(g p t) -> p g t", p=P, t=PACK))
+
+        def load_scales(plane, scales):
+            src = scales.bitcast(I32)
+            for q in range(4):
+                nc.sync.dma_start(
+                    out=plane[32 * q : 32 * q + 4, :, :].bitcast(I32),
+                    in_=src[:, 4 * q : 4 * q + 4, :].rearrange("g r n -> r g n"),
+                )
+
+        def load_x(g, h):
+            cols = slice(h * 2 * HALF, (h + 1) * 2 * HALF)
+            nc.sync.dma_start(out=x_codes[:, g, cols], in_=x_words[g, :, cols])
+
+        nc.sync.dma_start(out=w_raw[:, 0, :], in_=w_words[0])
+        load_x(0, 0)
+        load_scales(w_sraw, w_scales)
+        load_scales(x_sc, x_scales)
+        for g in range(1, KG):
+            nc.sync.dma_start(out=w_raw[:, g, :], in_=w_words[g])
+            load_x(g, 0)
+        for g in range(FG):
+            nc.sync.dma_start(
+                out=v_raw[g][:],
+                in_=v[512 * g : 512 * (g + 1), :].rearrange("(p j) n -> p j n", j=PACK),
+            )
+        for g in range(KG):
+            load_x(g, 1)
+        load_scales(c_sc, c_scales)
+        for g in range(FG):
+            nc.sync.dma_start(out=c_codes[:, g, :], in_=c_words[g].rearrange("p n t -> p (n t)"))
+
+        def sort_w(g, G):
+            nc.vector.tensor_copy(
+                out=w_sc[:, g, G],
+                in_=w_sraw[:, g, 512 * G : 512 * (G + 1)].rearrange("p (m t) -> p t m", t=PACK),
+            )
+            nc.vector.tensor_copy(
+                out=w_codes[:, g, G].rearrange("p t (m b) -> p t m b", b=2),
+                in_=w_raw[:, g, 1024 * G : 1024 * (G + 1)].rearrange("p (m t b) -> p t m b", t=PACK, b=2),
+            )
+
+        def first_pass(bank, h, G, t, g):
+            nc.tensor.matmul_mx(
+                out=bank[:],
+                lhsT=w_codes[:, g, G, t, :].bitcast(FP4X4),
+                lhsT_scale=w_sc[:, g, G, t, :],
+                rhs=x_codes[:, g, 2 * HALF * h : 2 * HALF * (h + 1)].bitcast(FP4X4),
+                rhs_scale=x_sc[:, g, HALF * h : HALF * (h + 1)],
+                start=(g == 0),
+                stop=(g == KG - 1),
+            )
+
+        def first_tile(h, G, t):
+            bank = psum.tile([P, HALF], F32, name="bank")
+            for g in range(KG):
+                first_pass(bank, h, G, t, g)
+            return bank
+
+        def hidden(bank, h_rows, G, t):
+            nc.scalar.activation(
+                out=h_rows[:, t, :], in_=bank[:], func=ACT.Relu, bias=b_col[:, G, t : t + 1]
+            )
+
+        def pack_hidden(h_rows, h_pack, part):
+            cols = slice(256 * part, 256 * (part + 1))
+            nc.vector.tensor_copy(
+                out=h_pack[:, cols, :], in_=h_rows[:, :, cols].rearrange("p t m -> p m t")
+            )
+
+        def quantize_hidden(h_pack, h, G, part):
+            cols = slice(256 * part, 256 * (part + 1))
+            nc.vector.quantize_mx(
+                out=h_codes[:, h, G, cols].bitcast(FP8X4),
+                scales=h_sc[:, h, G, cols],
+                in_=h_pack[:, cols, :].rearrange("p m t -> p (m t)"),
+            )
+
+        def pack_v(engine_copy, G, n, part, parts):
+            w = HALF // parts
+            dst = slice(w * part, w * (part + 1))
+            src = slice(HALF * n + w * part, HALF * n + w * (part + 1))
+            engine_copy(out=v_pack[G][n][:, dst, :], in_=v_raw[G][:, :, src].rearrange("p j n -> p n j"))
+
+        def quantize_v(G, n):
+            cols = slice(HALF * n, HALF * (n + 1))
+            nc.vector.quantize_mx(
+                out=v_codes[:, G, cols].bitcast(FP8X4),
+                scales=v_sc[:, G, cols],
+                in_=v_pack[G][n][:].rearrange("p m t -> p (m t)"),
+            )
+
+        def new_hidden():
+            h_rows = stage.tile([P, PACK, HALF], BF16, align_bytes=64, name="h_rows")
+            h_pack = stage.tile([P, HALF, PACK], BF16, align_bytes=64, name="h_pack")
+            return h_rows, h_pack
+
+        def head_matmul(i, codes, scales, n):
+            bank = psum.tile([P, HALF], F32, name="bank")
+            h, col = divmod(i * USERS, HALF)
+            for G in range(FG):
+                nc.tensor.matmul_mx(
+                    out=bank[:],
+                    lhsT=h_codes[:, h, G, col : col + USERS].bitcast(FP8X4),
+                    lhsT_scale=h_sc[:, h, G, col : col + USERS],
+                    rhs=codes(G, n),
+                    rhs_scale=scales[:, G, HALF * n : HALF * (n + 1)],
+                    start=(G == 0),
+                    stop=(G == FG - 1),
+                )
+            return bank
+
+        def c_view(G, n):
+            return c_codes[:, G, 4 * HALF * n : 4 * HALF * (n + 1)].bitcast(FP8X4)
+
+        def v_view(G, n):
+            return v_codes[:, G, HALF * n : HALF * (n + 1)].bitcast(FP8X4)
+
+        def score_matmuls(i):
+            banks = []
+            for n in range(2):
+                banks.append(head_matmul(i, c_view, c_sc, n))
+                banks.append(head_matmul(i, v_view, v_sc, n))
+            return banks
+
+        def score_out(i, banks):
+            rows = slice(USERS * i, USERS * (i + 1))
+            last = i == M // USERS - 1
+            p_click = outs.tile([P, N], F32, name="p_click")
+            p_conv = outs.tile([P, N], F32, name="p_conv")
+            p_both = outs.tile([P, N], F32, name="p_both")
+            for n in range(2):
+                cols = slice(HALF * n, HALF * (n + 1))
+                nc.scalar.activation(out=p_click[:, cols], in_=banks[2 * n][:], func=ACT.Sigmoid)
+                nc.scalar.activation(out=p_conv[:, cols], in_=banks[2 * n + 1][:], func=ACT.Sigmoid)
+                nc.vector.tensor_mul(p_both[:, cols], p_click[:, cols], p_conv[:, cols])
+                if last:
+                    nc.sync.dma_start(out=out_0[rows, cols], in_=p_click[:, cols])
+                    nc.sync.dma_start(out=out_1[rows, cols], in_=p_both[:, cols])
+            if not last:
+                nc.sync.dma_start(out=out_0[rows, :], in_=p_click[:])
+                nc.sync.dma_start(out=out_1[rows, :], in_=p_both[:])
+
+        hr0, hp0 = new_hidden()
+        hr1, hp1 = new_hidden()
+        hr2, hp2 = new_hidden()
+        banks = [psum.tile([P, HALF], F32, name="bank") for t in range(PACK)]
+        for g in range(KG):
+            sort_w(g, 0)
+            for t in range(PACK):
+                first_pass(banks[t], 0, 0, t, g)
+        for part in range(2):
+            pack_v(nc.scalar.copy, 0, 0, part, 2)
+        for t in range(PACK):
+            hidden(banks[t], hr0, 0, t)
+        banks = [psum.tile([P, HALF], F32, name="bank") for t in range(PACK)]
+        for g in range(KG):
+            sort_w(g, 1)
+            for t in range(PACK):
+                first_pass(banks[t], 0, 1, t, g)
+        pack_v(nc.vector.tensor_copy, 0, 1, 0, 1)
+        pack_v(nc.vector.tensor_copy, 1, 1, 0, 1)
+        quantize_v(0, 0)
+        quantize_v(0, 1)
+        pack_hidden(hr0, hp0, 0)
+        pack_hidden(hr0, hp0, 1)
+        quantize_v(1, 1)
+        quantize_hidden(hp0, 0, 0, 0)
+        quantize_hidden(hp0, 0, 0, 1)
+
+        for t in range(PACK):
+            hidden(banks[t], hr1, 1, t)
+        b0 = first_tile(1, 0, 0)
+        b1 = first_tile(1, 0, 1)
+        hidden(b0, hr2, 0, 0)
+        pack_v(nc.scalar.copy, 1, 0, 0, 2)
+        b2 = first_tile(1, 0, 2)
+        hidden(b1, hr2, 0, 1)
+        pack_v(nc.scalar.copy, 1, 0, 1, 2)
+        b3 = first_tile(1, 0, 3)
+        pack_hidden(hr1, hp1, 0)
+        pack_hidden(hr1, hp1, 1)
+        quantize_hidden(hp1, 0, 1, 0)
+        quantize_hidden(hp1, 0, 1, 1)
+        quantize_v(1, 0)
+        hidden(b2, hr2, 0, 2)
+        hidden(b3, hr2, 0, 3)
+        hr3, hp3 = new_hidden()
+        b0 = first_tile(1, 1, 0)
+        b1 = first_tile(1, 1, 1)
+        hidden(b0, hr3, 1, 0)
+        s0 = score_matmuls(0)
+        hidden(b1, hr3, 1, 1)
+        pack_hidden(hr2, hp2, 0)
+        pack_hidden(hr2, hp2, 1)
+        quantize_hidden(hp2, 1, 0, 0)
+        quantize_hidden(hp2, 1, 0, 1)
+        score_out(0, s0)
+        b2 = first_tile(1, 1, 2)
+        s1 = score_matmuls(1)
+        hidden(b2, hr3, 1, 2)
+        b3 = first_tile(1, 1, 3)
+        score_out(1, s1)
+        hidden(b3, hr3, 1, 3)
+        s2 = score_matmuls(2)
+        pack_hidden(hr3, hp3, 0)
+        pack_hidden(hr3, hp3, 1)
+        quantize_hidden(hp3, 1, 1, 0)
+        quantize_hidden(hp3, 1, 1, 1)
+        score_out(2, s2)
+        for i in range(3, M // USERS):
+            score_out(i, score_matmuls(i))

@@ -16,10 +16,14 @@ ACT = mybir.ActivationFunctionType
 
 P = 128
 PACK = 4
-KG = K // 512
-FG = F // 512
+PASS = P * PACK
+KG = K // PASS
+FG = F // PASS
 HALF = 512
+QUARTER = 256
 USERS = 128
+LAST = M // USERS - 1
+CHUNKS = ((0, 512), (512, 256), (768, 256))
 
 
 def tile_entire_space_conversion_s4_kernel(
@@ -29,118 +33,144 @@ def tile_entire_space_conversion_s4_kernel(
     with ExitStack() as ctx:
         keep = ctx.enter_context(tc.tile_pool(name="keep", bufs=1))
         stage = ctx.enter_context(tc.tile_pool(name="stage", bufs=3))
-        outs = ctx.enter_context(tc.tile_pool(name="outs", bufs=4))
+        outs = ctx.enter_context(tc.tile_pool(name="outs", bufs=5))
         psum = ctx.enter_context(tc.psum_pool(name="psum", bufs=8))
         ctx.enter_context(tc.manual_schedule())
 
-        w_raw = keep.tile([P, KG, 2 * F], U8, align_bytes=64, name="w_raw")
-        w_codes = keep.tile([P, KG, FG, PACK, 2 * P], U8, align_bytes=64, name="w_codes")
-        w_sraw = keep.tile([P, KG, F], U8, align_bytes=64, name="w_sraw")
-        w_sc = keep.tile([P, KG, FG, PACK, P], U8, align_bytes=64, name="w_sc")
-        x_codes = keep.tile([P, KG, 2 * M], U8, align_bytes=64, name="x_codes")
-        x_sc = keep.tile([P, KG, M], U8, align_bytes=64, name="x_sc")
-        c_codes = keep.tile([P, FG, 4 * N], U8, align_bytes=64, name="c_codes")
-        c_sc = keep.tile([P, FG, N], U8, align_bytes=64, name="c_sc")
-        v_raw = [keep.tile([P, PACK, N], BF16, align_bytes=64, name="v_raw%d" % g) for g in range(FG)]
-        v_pack = [
-            [keep.tile([P, HALF, PACK], BF16, align_bytes=64, name="v_pack%d%d" % (g, n)) for n in range(2)]
-            for g in range(FG)
-        ]
-        v_codes = keep.tile([P, FG, N], U32, align_bytes=64, name="v_codes")
-        v_sc = keep.tile([P, FG, N], U8, align_bytes=64, name="v_sc")
-        h_codes = keep.tile([P, 2, FG, HALF], U32, align_bytes=64, name="h_codes")
-        h_sc = keep.tile([P, 2, FG, HALF], U8, align_bytes=64, name="h_sc")
-        b_col = keep.tile([P, FG, PACK], BF16, align_bytes=64, name="b_col")
-        warm = keep.tile([P, 1], F32, name="warm")
+        def kept(shape, dtype, name):
+            return keep.tile(shape, dtype, align_bytes=64, name=name)
 
-        nc.vector.memset(warm[:], 0.0)
-        nc.scalar.activation(out=warm[:], in_=warm[:], func=ACT.Sigmoid)
-        nc.vector.memset(w_sraw[:].rearrange("p g n -> p (g n)").bitcast(I32), 0)
-        nc.gpsimd.memset(x_sc[:].rearrange("p g n -> p (g n)").bitcast(I32), 0)
-        nc.gpsimd.memset(c_sc[:].rearrange("p g n -> p (g n)").bitcast(I32), 0)
-        nc.gpsimd.dma_start(out=b_col[:], in_=b.rearrange("(g p t) -> p g t", p=P, t=PACK))
+        w_raw = [kept([P, KG, 2 * PASS], U8, "w_raw%d" % G) for G in range(FG)]
+        w_raw_sc = [kept([P, KG, PASS], U8, "w_raw_sc%d" % G) for G in range(FG)]
+        w_codes = kept([P, KG, FG, PACK, 2 * P], U8, "w_codes")
+        w_sc = kept([P, KG, FG, PACK, P], U8, "w_sc")
+        x_codes = [kept([P, KG, 2 * HALF], U8, "x_codes%d" % h) for h in range(2)]
+        x_sc = [kept([P, KG, HALF], U8, "x_sc%d" % h) for h in range(2)]
+        c_codes = kept([P, FG, 4 * N], U8, "c_codes")
+        c_sc = kept([P, FG, N], U8, "c_sc")
+        v_raw = [[kept([P, PACK, HALF], BF16, "v_raw%d%d" % (G, n)) for n in range(2)] for G in range(FG)]
+        v_pack = [[kept([P, HALF, PACK], BF16, "v_pack%d%d" % (G, n)) for n in range(2)] for G in range(FG)]
+        v_codes = kept([P, FG, N], U32, "v_codes")
+        v_sc = kept([P, FG, N], U8, "v_sc")
+        h_codes = kept([P, FG, M], U32, "h_codes")
+        h_sc = kept([P, FG, M], U8, "h_sc")
+        b_col = kept([P, FG, PACK], BF16, "b_col")
+        warm = kept([P, 1], F32, "warm")
 
-        def load_scales(plane, scales):
-            src = scales.bitcast(I32)
+        def fill(engine, tile):
+            engine.memset(tile[:].bitcast(I32), 0)
+
+        def load_scales(tile, scales, lo, hi):
+            rows = scales.bitcast(I32)
             for q in range(4):
                 nc.sync.dma_start(
-                    out=plane[32 * q : 32 * q + 4, :, :].bitcast(I32),
-                    in_=src[:, 4 * q : 4 * q + 4, :].rearrange("g r n -> r g n"),
+                    out=tile[32 * q : 32 * q + 4, :, :].bitcast(I32),
+                    in_=rows[:, 4 * q : 4 * q + 4, lo // 4 : hi // 4].rearrange("g r n -> r g n"),
                 )
 
-        def load_x(g, h):
-            cols = slice(h * 2 * HALF, (h + 1) * 2 * HALF)
-            nc.sync.dma_start(out=x_codes[:, g, cols], in_=x_words[g, :, cols])
-
-        nc.sync.dma_start(out=w_raw[:, 0, :], in_=w_words[0])
-        load_x(0, 0)
-        load_scales(w_sraw, w_scales)
-        load_scales(x_sc, x_scales)
-        for g in range(1, KG):
-            nc.sync.dma_start(out=w_raw[:, g, :], in_=w_words[g])
-            load_x(g, 0)
-        for g in range(FG):
+        def load_words(tile, words, g, count, part):
+            cols = slice(2 * PASS * part, 2 * PASS * (part + 1))
             nc.sync.dma_start(
-                out=v_raw[g][:],
-                in_=v[512 * g : 512 * (g + 1), :].rearrange("(p j) n -> p j n", j=PACK),
+                out=tile[:, g : g + count, :], in_=words[g : g + count, :, cols].rearrange("g p n -> p g n")
             )
-        for g in range(KG):
-            load_x(g, 1)
-        load_scales(c_sc, c_scales)
-        for g in range(FG):
-            nc.sync.dma_start(out=c_codes[:, g, :], in_=c_words[g].rearrange("p n t -> p (n t)"))
+
+        def load_v(G, n):
+            nc.sync.dma_start(
+                out=v_raw[G][n][:],
+                in_=v[PASS * G : PASS * (G + 1), HALF * n : HALF * (n + 1)].rearrange("(p j) n -> p j n", j=PACK),
+            )
+
+        nc.gpsimd.dma_start(out=b_col[:], in_=b.rearrange("(g p t) -> p g t", p=P, t=PACK))
+        fill(nc.vector, w_raw_sc[0])
+        fill(nc.vector, x_sc[0])
+        fill(nc.vector, w_raw_sc[1])
+        nc.vector.memset(warm[:], 0.0)
+        nc.scalar.activation(out=warm[:], in_=warm[:], func=ACT.Sigmoid)
+        fill(nc.gpsimd, x_sc[1])
+        fill(nc.gpsimd, c_sc)
+
+        load_words(w_raw[0], w_words, 0, 1, 0)
+        load_words(x_codes[0], x_words, 0, 1, 0)
+        load_scales(w_raw_sc[0], w_scales, 0, PASS)
+        load_scales(x_sc[0], x_scales, 0, HALF)
+        for g in range(1, KG):
+            load_words(w_raw[0], w_words, g, 1, 0)
+            load_words(x_codes[0], x_words, g, 1, 0)
+        load_v(0, 0)
+        load_words(w_raw[1], w_words, 0, KG, 1)
+        load_scales(w_raw_sc[1], w_scales, PASS, F)
+        load_v(0, 1)
+        load_v(1, 0)
+        load_v(1, 1)
+        load_scales(x_sc[1], x_scales, HALF, M)
+        load_words(x_codes[1], x_words, 0, KG, 1)
+        load_scales(c_sc, c_scales, 0, N)
+        for G in range(FG):
+            nc.sync.dma_start(out=c_codes[:, G, :], in_=c_words[G].rearrange("p n t -> p (n t)"))
 
         def sort_w(g, G):
             nc.vector.tensor_copy(
-                out=w_sc[:, g, G],
-                in_=w_sraw[:, g, 512 * G : 512 * (G + 1)].rearrange("p (m t) -> p t m", t=PACK),
+                out=w_sc[:, g, G], in_=w_raw_sc[G][:, g, :].rearrange("p (m t) -> p t m", t=PACK)
             )
             nc.vector.tensor_copy(
                 out=w_codes[:, g, G].rearrange("p t (m b) -> p t m b", b=2),
-                in_=w_raw[:, g, 1024 * G : 1024 * (G + 1)].rearrange("p (m t b) -> p t m b", t=PACK, b=2),
+                in_=w_raw[G][:, g, :].rearrange("p (m t b) -> p t m b", t=PACK, b=2),
             )
 
-        def first_pass(bank, h, G, t, g):
+        def interleave(copy, out, rows):
+            copy(
+                out=out.rearrange("p (c i) t -> p c t i", i=4), in_=rows.rearrange("p t (c i) -> p c t i", i=4)
+            )
+
+        def new_banks(count=PACK):
+            return [psum.tile([P, HALF], F32, name="bank") for t in range(count)]
+
+        def hidden_pass(bank, chunk, G, t, g):
+            start, width = CHUNKS[chunk]
+            h, col = divmod(start, HALF)
             nc.tensor.matmul_mx(
-                out=bank[:],
+                out=bank[:, 0:width],
                 lhsT=w_codes[:, g, G, t, :].bitcast(FP4X4),
                 lhsT_scale=w_sc[:, g, G, t, :],
-                rhs=x_codes[:, g, 2 * HALF * h : 2 * HALF * (h + 1)].bitcast(FP4X4),
-                rhs_scale=x_sc[:, g, HALF * h : HALF * (h + 1)],
+                rhs=x_codes[h][:, g, 2 * col : 2 * (col + width)].bitcast(FP4X4),
+                rhs_scale=x_sc[h][:, g, col : col + width],
                 start=(g == 0),
                 stop=(g == KG - 1),
             )
 
-        def first_tile(h, G, t):
-            bank = psum.tile([P, HALF], F32, name="bank")
-            for g in range(KG):
-                first_pass(bank, h, G, t, g)
-            return bank
+        def hidden_matmuls(chunk, G, ts):
+            banks = new_banks(len(ts))
+            for t, bank in zip(ts, banks):
+                for g in range(KG):
+                    hidden_pass(bank, chunk, G, t, g)
+            return banks
 
-        def hidden(bank, h_rows, G, t):
-            nc.scalar.activation(
-                out=h_rows[:, t, :], in_=bank[:], func=ACT.Relu, bias=b_col[:, G, t : t + 1]
-            )
+        def relu_out(banks, rows, chunk, G, ts):
+            width = CHUNKS[chunk][1]
+            for t, bank in zip(ts, banks):
+                nc.scalar.activation(
+                    out=rows[:, t, 0:width], in_=bank[:, 0:width], func=ACT.Relu, bias=b_col[:, G, t : t + 1]
+                )
 
-        def pack_hidden(h_rows, h_pack, part):
-            cols = slice(256 * part, 256 * (part + 1))
-            nc.vector.tensor_copy(
-                out=h_pack[:, cols, :], in_=h_rows[:, :, cols].rearrange("p t m -> p m t")
-            )
+        def quantize_hidden(rows, chunk, G):
+            start, width = CHUNKS[chunk]
+            packed = stage.tile([P, HALF, PACK], BF16, align_bytes=64, name="packed")
+            cuts = [slice(lo, lo + QUARTER) for lo in range(0, width, QUARTER)]
+            for cut in cuts:
+                interleave(nc.vector.tensor_copy, packed[:, cut, :], rows[:, :, cut])
+            for cut in cuts:
+                users = slice(start + cut.start, start + cut.stop)
+                nc.vector.quantize_mx(
+                    out=h_codes[:, G, users].bitcast(FP8X4),
+                    scales=h_sc[:, G, users],
+                    in_=packed[:, cut, :].rearrange("p m t -> p (m t)"),
+                )
 
-        def quantize_hidden(h_pack, h, G, part):
-            cols = slice(256 * part, 256 * (part + 1))
-            nc.vector.quantize_mx(
-                out=h_codes[:, h, G, cols].bitcast(FP8X4),
-                scales=h_sc[:, h, G, cols],
-                in_=h_pack[:, cols, :].rearrange("p m t -> p (m t)"),
-            )
+        def new_rows():
+            return stage.tile([P, PACK, HALF], BF16, align_bytes=64, name="rows")
 
-        def pack_v(engine_copy, G, n, part, parts):
-            w = HALF // parts
-            dst = slice(w * part, w * (part + 1))
-            src = slice(HALF * n + w * part, HALF * n + w * (part + 1))
-            engine_copy(out=v_pack[G][n][:, dst, :], in_=v_raw[G][:, :, src].rearrange("p j n -> p n j"))
+        def pack_v(copy, G, n, lo, hi):
+            interleave(copy, v_pack[G][n][:, lo:hi, :], v_raw[G][n][:, :, lo:hi])
 
         def quantize_v(G, n):
             cols = slice(HALF * n, HALF * (n + 1))
@@ -150,123 +180,147 @@ def tile_entire_space_conversion_s4_kernel(
                 in_=v_pack[G][n][:].rearrange("p m t -> p (m t)"),
             )
 
-        def new_hidden():
-            h_rows = stage.tile([P, PACK, HALF], BF16, align_bytes=64, name="h_rows")
-            h_pack = stage.tile([P, HALF, PACK], BF16, align_bytes=64, name="h_pack")
-            return h_rows, h_pack
-
-        def head_matmul(i, codes, scales, n):
+        def score_matmul(i, codes, scales, lo, width):
             bank = psum.tile([P, HALF], F32, name="bank")
-            h, col = divmod(i * USERS, HALF)
+            users = slice(USERS * i, USERS * (i + 1))
             for G in range(FG):
                 nc.tensor.matmul_mx(
-                    out=bank[:],
-                    lhsT=h_codes[:, h, G, col : col + USERS].bitcast(FP8X4),
-                    lhsT_scale=h_sc[:, h, G, col : col + USERS],
-                    rhs=codes(G, n),
-                    rhs_scale=scales[:, G, HALF * n : HALF * (n + 1)],
+                    out=bank[:, 0:width],
+                    lhsT=h_codes[:, G, users].bitcast(FP8X4),
+                    lhsT_scale=h_sc[:, G, users],
+                    rhs=codes(G, lo, lo + width),
+                    rhs_scale=scales[:, G, lo : lo + width],
                     start=(G == 0),
                     stop=(G == FG - 1),
                 )
             return bank
 
-        def c_view(G, n):
-            return c_codes[:, G, 4 * HALF * n : 4 * HALF * (n + 1)].bitcast(FP8X4)
+        def c_view(G, lo, hi):
+            return c_codes[:, G, 4 * lo : 4 * hi].bitcast(FP8X4)
 
-        def v_view(G, n):
-            return v_codes[:, G, HALF * n : HALF * (n + 1)].bitcast(FP8X4)
+        def v_view(G, lo, hi):
+            return v_codes[:, G, lo:hi].bitcast(FP8X4)
 
-        def score_matmuls(i):
-            banks = []
-            for n in range(2):
-                banks.append(head_matmul(i, c_view, c_sc, n))
-                banks.append(head_matmul(i, v_view, v_sc, n))
-            return banks
+        HALVES = ((0, HALF), (HALF, HALF))
 
-        def score_out(i, banks):
-            rows = slice(USERS * i, USERS * (i + 1))
-            last = i == M // USERS - 1
-            p_click = outs.tile([P, N], F32, name="p_click")
-            p_conv = outs.tile([P, N], F32, name="p_conv")
-            p_both = outs.tile([P, N], F32, name="p_both")
-            for n in range(2):
-                cols = slice(HALF * n, HALF * (n + 1))
-                nc.scalar.activation(out=p_click[:, cols], in_=banks[2 * n][:], func=ACT.Sigmoid)
-                nc.scalar.activation(out=p_conv[:, cols], in_=banks[2 * n + 1][:], func=ACT.Sigmoid)
+        def click_matmuls(i, parts=HALVES):
+            return [score_matmul(i, c_view, c_sc, lo, width) for lo, width in parts]
+
+        def conv_matmuls(i, parts=HALVES):
+            return [score_matmul(i, v_view, v_sc, lo, width) for lo, width in parts]
+
+        def new_out(name):
+            return outs.tile([P, N], F32, name=name)
+
+        def sigmoids(out, banks, parts):
+            for (lo, width), bank in zip(parts, banks):
+                nc.scalar.activation(out=out[:, lo : lo + width], in_=bank[:, 0:width], func=ACT.Sigmoid)
+
+        def store(dram, i, tile, lo=0, hi=N):
+            nc.sync.dma_start(out=dram[USERS * i : USERS * (i + 1), lo:hi], in_=tile[:, lo:hi])
+
+        def click_out(i, banks):
+            p_click = new_out("p_click")
+            sigmoids(p_click, banks, HALVES)
+            store(out_0, i, p_click)
+            return p_click
+
+        def conv_part(banks, parts, p_click, p_conv, p_both):
+            for (lo, width), bank in zip(parts, banks):
+                cols = slice(lo, lo + width)
+                sigmoids(p_conv, [bank], [(lo, width)])
                 nc.vector.tensor_mul(p_both[:, cols], p_click[:, cols], p_conv[:, cols])
-                if last:
-                    nc.sync.dma_start(out=out_0[rows, cols], in_=p_click[:, cols])
-                    nc.sync.dma_start(out=out_1[rows, cols], in_=p_both[:, cols])
-            if not last:
-                nc.sync.dma_start(out=out_0[rows, :], in_=p_click[:])
-                nc.sync.dma_start(out=out_1[rows, :], in_=p_both[:])
 
-        hr0, hp0 = new_hidden()
-        hr1, hp1 = new_hidden()
-        hr2, hp2 = new_hidden()
-        banks = [psum.tile([P, HALF], F32, name="bank") for t in range(PACK)]
+        def conv_out(i, banks, p_click):
+            p_conv = new_out("p_conv")
+            p_both = new_out("p_both")
+            conv_part(banks, HALVES, p_click, p_conv, p_both)
+            store(out_1, i, p_both)
+
+        def last_scores(i):
+            click = new_out("p_click")
+            conv = new_out("p_conv")
+            both = new_out("p_both")
+            steps = []
+            for click_part, conv_parts in (
+                ((0, HALF), ((0, HALF),)),
+                ((HALF, HALF), ((HALF, QUARTER), (HALF + QUARTER, QUARTER))),
+            ):
+                steps.append((click_part, click_matmuls(i, [click_part]), conv_parts, conv_matmuls(i, conv_parts)))
+            for click_part, click_banks, conv_parts, conv_banks in steps:
+                sigmoids(click, click_banks, [click_part])
+                store(out_0, i, click, click_part[0], click_part[0] + click_part[1])
+                for part, bank in zip(conv_parts, conv_banks):
+                    conv_part([bank], [part], click, conv, both)
+                    store(out_1, i, both, part[0], part[0] + part[1])
+
+        every = range(PACK)
+        banks = new_banks()
         for g in range(KG):
             sort_w(g, 0)
-            for t in range(PACK):
-                first_pass(banks[t], 0, 0, t, g)
-        for part in range(2):
-            pack_v(nc.scalar.copy, 0, 0, part, 2)
-        for t in range(PACK):
-            hidden(banks[t], hr0, 0, t)
-        banks = [psum.tile([P, HALF], F32, name="bank") for t in range(PACK)]
+            for t in every:
+                hidden_pass(banks[t], 0, 0, t, g)
+        pack_v(nc.scalar.copy, 0, 0, 0, 256)
+        pack_v(nc.scalar.copy, 0, 0, 256, 512)
+        rows = new_rows()
+        relu_out(banks, rows, 0, 0, every)
+        banks = new_banks()
         for g in range(KG):
             sort_w(g, 1)
-            for t in range(PACK):
-                first_pass(banks[t], 0, 1, t, g)
-        pack_v(nc.vector.tensor_copy, 0, 1, 0, 1)
-        pack_v(nc.vector.tensor_copy, 1, 1, 0, 1)
+            for t in every:
+                hidden_pass(banks[t], 0, 1, t, g)
+        pack_v(nc.scalar.copy, 0, 1, 0, 256)
+        pack_v(nc.vector.tensor_copy, 1, 0, 0, 512)
+        quantize_hidden(rows, 0, 0)
         quantize_v(0, 0)
-        quantize_v(0, 1)
-        pack_hidden(hr0, hp0, 0)
-        pack_hidden(hr0, hp0, 1)
-        quantize_v(1, 1)
-        quantize_hidden(hp0, 0, 0, 0)
-        quantize_hidden(hp0, 0, 0, 1)
+        rows = new_rows()
+        relu_out(banks, rows, 0, 1, every)
+        quantize_hidden(rows, 0, 1)
+        pack_v(nc.scalar.copy, 0, 1, 256, 512)
 
-        for t in range(PACK):
-            hidden(banks[t], hr1, 1, t)
-        b0 = first_tile(1, 0, 0)
-        b1 = first_tile(1, 0, 1)
-        hidden(b0, hr2, 0, 0)
-        pack_v(nc.scalar.copy, 1, 0, 0, 2)
-        b2 = first_tile(1, 0, 2)
-        hidden(b1, hr2, 0, 1)
-        pack_v(nc.scalar.copy, 1, 0, 1, 2)
-        b3 = first_tile(1, 0, 3)
-        pack_hidden(hr1, hp1, 0)
-        pack_hidden(hr1, hp1, 1)
-        quantize_hidden(hp1, 0, 1, 0)
-        quantize_hidden(hp1, 0, 1, 1)
+        banks = hidden_matmuls(1, 0, every)
+        rows_10 = new_rows()
+        relu_out(banks, rows_10, 1, 0, every)
+        pack_v(nc.vector.tensor_copy, 1, 1, 0, 512)
         quantize_v(1, 0)
-        hidden(b2, hr2, 0, 2)
-        hidden(b3, hr2, 0, 3)
-        hr3, hp3 = new_hidden()
-        b0 = first_tile(1, 1, 0)
-        b1 = first_tile(1, 1, 1)
-        hidden(b0, hr3, 1, 0)
-        s0 = score_matmuls(0)
-        hidden(b1, hr3, 1, 1)
-        pack_hidden(hr2, hp2, 0)
-        pack_hidden(hr2, hp2, 1)
-        quantize_hidden(hp2, 1, 0, 0)
-        quantize_hidden(hp2, 1, 0, 1)
-        score_out(0, s0)
-        b2 = first_tile(1, 1, 2)
-        s1 = score_matmuls(1)
-        hidden(b2, hr3, 1, 2)
-        b3 = first_tile(1, 1, 3)
-        score_out(1, s1)
-        hidden(b3, hr3, 1, 3)
-        s2 = score_matmuls(2)
-        pack_hidden(hr3, hp3, 0)
-        pack_hidden(hr3, hp3, 1)
-        quantize_hidden(hp3, 1, 1, 0)
-        quantize_hidden(hp3, 1, 1, 1)
-        score_out(2, s2)
-        for i in range(3, M // USERS):
-            score_out(i, score_matmuls(i))
+        banks = hidden_matmuls(1, 1, every)
+        click_0 = click_matmuls(0)
+        rows_11 = new_rows()
+        relu_out(banks, rows_11, 1, 1, every)
+        quantize_v(0, 1)
+        quantize_v(1, 1)
+        quantize_hidden(rows_10, 1, 0)
+        p_click_0 = click_out(0, click_0)
+        click_1 = click_matmuls(1)
+        p_click_1 = click_out(1, click_1)
+        quantize_hidden(rows_11, 1, 1)
+        rows_20 = new_rows()
+        banks = hidden_matmuls(2, 0, (0, 1))
+        conv = conv_matmuls(0)
+        relu_out(banks, rows_20, 2, 0, (0, 1))
+        conv_out(0, conv, p_click_0)
+        banks = hidden_matmuls(2, 0, (2, 3))
+        conv = conv_matmuls(1)
+        relu_out(banks, rows_20, 2, 0, (2, 3))
+        conv_out(1, conv, p_click_1)
+        click = click_matmuls(2)
+        p_click = click_out(2, click)
+        quantize_hidden(rows_20, 2, 0)
+        conv = conv_matmuls(2)
+        conv_out(2, conv, p_click)
+        rows_21 = new_rows()
+        for i, ts in ((3, (0, 1)), (4, (2, 3))):
+            banks = hidden_matmuls(2, 1, ts)
+            click = click_matmuls(i)
+            relu_out(banks, rows_21, 2, 1, ts)
+            p_click = click_out(i, click)
+            if i == 4:
+                quantize_hidden(rows_21, 2, 1)
+            conv = conv_matmuls(i)
+            conv_out(i, conv, p_click)
+        for i in range(5, LAST):
+            click = click_matmuls(i)
+            p_click = click_out(i, click)
+            conv = conv_matmuls(i)
+            conv_out(i, conv, p_click)
+        last_scores(LAST)

@@ -68,10 +68,11 @@ def tile_entire_space_conversion_s4_kernel(
                     in_=rows[:, 4 * q : 4 * q + 4, lo // 4 : hi // 4].rearrange("g r n -> r g n"),
                 )
 
-        def load_words(tile, words, g, count, part):
+        def load_words(tile, words, g, count, part, engine=nc.sync):
             cols = slice(2 * PASS * part, 2 * PASS * (part + 1))
-            nc.sync.dma_start(
-                out=tile[:, g : g + count, :], in_=words[g : g + count, :, cols].rearrange("g p n -> p g n")
+            engine.dma_start(
+                out=tile[:, g : g + count, :].bitcast(I32),
+                in_=words.bitcast(I32)[g : g + count, :, cols.start // 4 : cols.stop // 4].rearrange("g p n -> p g n"),
             )
 
         def load_v(G, n):
@@ -80,6 +81,7 @@ def tile_entire_space_conversion_s4_kernel(
                 in_=v[PASS * G : PASS * (G + 1), HALF * n : HALF * (n + 1)].rearrange("(p j) n -> p j n", j=PACK),
             )
 
+        load_words(w_raw[0], w_words, 0, 1, 0, nc.gpsimd)
         nc.gpsimd.dma_start(out=b_col[:], in_=b.rearrange("(g p t) -> p g t", p=P, t=PACK))
         fill(nc.vector, w_raw_sc[0])
         fill(nc.vector, x_sc[0])
@@ -89,7 +91,6 @@ def tile_entire_space_conversion_s4_kernel(
         fill(nc.gpsimd, x_sc[1])
         fill(nc.gpsimd, c_sc)
 
-        load_words(w_raw[0], w_words, 0, 1, 0)
         load_words(x_codes[0], x_words, 0, 1, 0)
         load_scales(w_raw_sc[0], w_scales, 0, PASS)
         load_scales(x_sc[0], x_scales, 0, HALF)

from contextlib import ExitStack

import concourse.mybir as mybir

M, K, F, N = 1024, 2048, 1024, 1024
FLOPS = 2 * M * K * F + 2 * 2 * M * F * N

F32 = mybir.dt.float32
BF16 = mybir.dt.bfloat16
I32 = mybir.dt.int32
U32 = mybir.dt.uint32
U8 = mybir.dt.uint8
FP8X4 = mybir.dt.float8_e4m3fn_x4
FP4X4 = mybir.dt.float4_e2m1fn_x4
ACT = mybir.ActivationFunctionType

P = 128
PACK = 4
PASS = P * PACK
KG = K // PASS
FG = F // PASS
HALF = 512
QUARTER = 256
USERS = 128
LAST = M // USERS - 1
CHUNKS = ((0, 512), (512, 256), (768, 256))


def tile_entire_space_conversion_s4_kernel(
    tc, x_words, x_scales, w_words, w_scales, b, c_words, c_scales, v, out_0, out_1
):
    nc = tc.nc
    with ExitStack() as ctx:
        keep = ctx.enter_context(tc.tile_pool(name="keep", bufs=1))
        stage = ctx.enter_context(tc.tile_pool(name="stage", bufs=3))
        outs = ctx.enter_context(tc.tile_pool(name="outs", bufs=5))
        psum = ctx.enter_context(tc.psum_pool(name="psum", bufs=8))
        ctx.enter_context(tc.manual_schedule())

        def kept(shape, dtype, name):
            return keep.tile(shape, dtype, align_bytes=64, name=name)

        w_raw = [kept([P, KG, 2 * PASS], U8, "w_raw%d" % G) for G in range(FG)]
        w_raw_sc = [kept([P, KG, PASS], U8, "w_raw_sc%d" % G) for G in range(FG)]
        w_codes = kept([P, KG, FG, PACK, 2 * P], U8, "w_codes")
        w_sc = kept([P, KG, FG, PACK, P], U8, "w_sc")
        x_codes = [kept([P, KG, 2 * HALF], U8, "x_codes%d" % h) for h in range(2)]
        x_sc = [kept([P, KG, HALF], U8, "x_sc%d" % h) for h in range(2)]
        c_codes = kept([P, FG, 4 * N], U8, "c_codes")
        c_sc = kept([P, FG, N], U8, "c_sc")
        v_raw = [[kept([P, PACK, HALF], BF16, "v_raw%d%d" % (G, n)) for n in range(2)] for G in range(FG)]
        v_pack = [[kept([P, HALF, PACK], BF16, "v_pack%d%d" % (G, n)) for n in range(2)] for G in range(FG)]
        v_codes = kept([P, FG, N], U32, "v_codes")
        v_sc = kept([P, FG, N], U8, "v_sc")
        h_codes = kept([P, FG, M], U32, "h_codes")
        h_sc = kept([P, FG, M], U8, "h_sc")
        b_col = kept([P, FG, PACK], BF16, "b_col")
        warm = kept([P, 1], F32, "warm")

        def fill(engine, tile):
            engine.memset(tile[:].bitcast(I32), 0)

        def load_scales(tile, scales, lo, hi):
            rows = scales.bitcast(I32)
            for q in range(4):
                nc.sync.dma_start(
                    out=tile[32 * q : 32 * q + 4, :, :].bitcast(I32),
                    in_=rows[:, 4 * q : 4 * q + 4, lo // 4 : hi // 4].rearrange("g r n -> r g n"),
                )

        def load_words(tile, words, g, count, part, engine=nc.sync):
            cols = slice(2 * PASS * part, 2 * PASS * (part + 1))
            engine.dma_start(
                out=tile[:, g : g + count, :].bitcast(I32),
                in_=words.bitcast(I32)[g : g + count, :, cols.start // 4 : cols.stop // 4].rearrange("g p n -> p g n"),
            )

        def load_v(G, n):
            nc.sync.dma_start(
                out=v_raw[G][n][:],
                in_=v[PASS * G : PASS * (G + 1), HALF * n : HALF * (n + 1)].rearrange("(p j) n -> p j n", j=PACK),
            )

        load_words(w_raw[0], w_words, 0, 1, 0, nc.gpsimd)
        nc.gpsimd.dma_start(out=b_col[:], in_=b.rearrange("(g p t) -> p g t", p=P, t=PACK))
        fill(nc.vector, w_raw_sc[0])
        fill(nc.vector, x_sc[0])
        fill(nc.vector, w_raw_sc[1])
        nc.vector.memset(warm[:], 0.0)
        nc.scalar.activation(out=warm[:], in_=warm[:], func=ACT.Sigmoid)
        fill(nc.gpsimd, x_sc[1])
        fill(nc.gpsimd, c_sc)

        load_words(x_codes[0], x_words, 0, 1, 0)
        load_scales(w_raw_sc[0], w_scales, 0, PASS)
        load_scales(x_sc[0], x_scales, 0, HALF)
        for g in range(1, KG):
            load_words(w_raw[0], w_words, g, 1, 0)
            load_words(x_codes[0], x_words, g, 1, 0)
        load_v(0, 0)
        load_words(w_raw[1], w_words, 0, KG, 1)
        load_scales(w_raw_sc[1], w_scales, PASS, F)
        load_v(0, 1)
        load_v(1, 0)
        load_v(1, 1)
        load_scales(x_sc[1], x_scales, HALF, M)
        load_words(x_codes[1], x_words, 0, KG, 1)
        load_scales(c_sc, c_scales, 0, N)
        for G in range(FG):
            nc.sync.dma_start(out=c_codes[:, G, :], in_=c_words[G].rearrange("p n t -> p (n t)"))

        def sort_w(g, G):
            nc.vector.tensor_copy(
                out=w_sc[:, g, G], in_=w_raw_sc[G][:, g, :].rearrange("p (m t) -> p t m", t=PACK)
            )
            nc.vector.tensor_copy(
                out=w_codes[:, g, G].rearrange("p t (m b) -> p t m b", b=2),
                in_=w_raw[G][:, g, :].rearrange("p (m t b) -> p t m b", t=PACK, b=2),
            )

        def interleave(copy, out, rows):
            copy(
                out=out.rearrange("p (c i) t -> p c t i", i=4), in_=rows.rearrange("p t (c i) -> p c t i", i=4)
            )

        def new_banks(count=PACK):
            return [psum.tile([P, HALF], F32, name="bank") for t in range(count)]

        def hidden_pass(bank, chunk, G, t, g):
            start, width = CHUNKS[chunk]
            h, col = divmod(start, HALF)
            nc.tensor.matmul_mx(
                out=bank[:, 0:width],
                lhsT=w_codes[:, g, G, t, :].bitcast(FP4X4),
                lhsT_scale=w_sc[:, g, G, t, :],
                rhs=x_codes[h][:, g, 2 * col : 2 * (col + width)].bitcast(FP4X4),
                rhs_scale=x_sc[h][:, g, col : col + width],
                start=(g == 0),
                stop=(g == KG - 1),
            )

        def hidden_matmuls(chunk, G, ts):
            banks = new_banks(len(ts))
            for t, bank in zip(ts, banks):
                for g in range(KG):
                    hidden_pass(bank, chunk, G, t, g)
            return banks

        def relu_out(banks, rows, chunk, G, ts):
            width = CHUNKS[chunk][1]
            for t, bank in zip(ts, banks):
                nc.scalar.activation(
                    out=rows[:, t, 0:width], in_=bank[:, 0:width], func=ACT.Relu, bias=b_col[:, G, t : t + 1]
                )

        def quantize_hidden(rows, chunk, G):
            start, width = CHUNKS[chunk]
            packed = stage.tile([P, HALF, PACK], BF16, align_bytes=64, name="packed")
            cuts = [slice(lo, lo + QUARTER) for lo in range(0, width, QUARTER)]
            for cut in cuts:
                interleave(nc.vector.tensor_copy, packed[:, cut, :], rows[:, :, cut])
            for cut in cuts:
                users = slice(start + cut.start, start + cut.stop)
                nc.vector.quantize_mx(
                    out=h_codes[:, G, users].bitcast(FP8X4),
                    scales=h_sc[:, G, users],
                    in_=packed[:, cut, :].rearrange("p m t -> p (m t)"),
                )

        def new_rows():
            return stage.tile([P, PACK, HALF], BF16, align_bytes=64, name="rows")

        def pack_v(copy, G, n, lo, hi):
            interleave(copy, v_pack[G][n][:, lo:hi, :], v_raw[G][n][:, :, lo:hi])

        def quantize_v(G, n):
            cols = slice(HALF * n, HALF * (n + 1))
            nc.vector.quantize_mx(
                out=v_codes[:, G, cols].bitcast(FP8X4),
                scales=v_sc[:, G, cols],
                in_=v_pack[G][n][:].rearrange("p m t -> p (m t)"),
            )

        def score_matmul(i, codes, scales, lo, width):
            bank = psum.tile([P, HALF], F32, name="bank")
            users = slice(USERS * i, USERS * (i + 1))
            for G in range(FG):
                nc.tensor.matmul_mx(
                    out=bank[:, 0:width],
                    lhsT=h_codes[:, G, users].bitcast(FP8X4),
                    lhsT_scale=h_sc[:, G, users],
                    rhs=codes(G, lo, lo + width),
                    rhs_scale=scales[:, G, lo : lo + width],
                    start=(G == 0),
                    stop=(G == FG - 1),
                )
            return bank

        def c_view(G, lo, hi):
            return c_codes[:, G, 4 * lo : 4 * hi].bitcast(FP8X4)

        def v_view(G, lo, hi):
            return v_codes[:, G, lo:hi].bitcast(FP8X4)

        HALVES = ((0, HALF), (HALF, HALF))

        def click_matmuls(i, parts=HALVES):
            return [score_matmul(i, c_view, c_sc, lo, width) for lo, width in parts]

        def conv_matmuls(i, parts=HALVES):
            return [score_matmul(i, v_view, v_sc, lo, width) for lo, width in parts]

        def new_out(name):
            return outs.tile([P, N], F32, name=name)

        def sigmoids(out, banks, parts):
            for (lo, width), bank in zip(parts, banks):
                nc.scalar.activation(out=out[:, lo : lo + width], in_=bank[:, 0:width], func=ACT.Sigmoid)

        def store(dram, i, tile, lo=0, hi=N):
            nc.sync.dma_start(out=dram[USERS * i : USERS * (i + 1), lo:hi], in_=tile[:, lo:hi])

        def click_out(i, banks):
            p_click = new_out("p_click")
            sigmoids(p_click, banks, HALVES)
            store(out_0, i, p_click)
            return p_click

        def conv_part(banks, parts, p_click, p_conv, p_both):
            for (lo, width), bank in zip(parts, banks):
                cols = slice(lo, lo + width)
                sigmoids(p_conv, [bank], [(lo, width)])
                nc.vector.tensor_mul(p_both[:, cols], p_click[:, cols], p_conv[:, cols])

        def conv_out(i, banks, p_click):
            p_conv = new_out("p_conv")
            p_both = new_out("p_both")
            conv_part(banks, HALVES, p_click, p_conv, p_both)
            store(out_1, i, p_both)

        def last_scores(i):
            click = new_out("p_click")
            conv = new_out("p_conv")
            both = new_out("p_both")
            steps = []
            for click_part, conv_parts in (
                ((0, HALF), ((0, HALF),)),
                ((HALF, HALF), ((HALF, QUARTER), (HALF + QUARTER, QUARTER))),
            ):
                steps.append((click_part, click_matmuls(i, [click_part]), conv_parts, conv_matmuls(i, conv_parts)))
            for click_part, click_banks, conv_parts, conv_banks in steps:
                sigmoids(click, click_banks, [click_part])
                store(out_0, i, click, click_part[0], click_part[0] + click_part[1])
                for part, bank in zip(conv_parts, conv_banks):
                    conv_part([bank], [part], click, conv, both)
                    store(out_1, i, both, part[0], part[0] + part[1])

        every = range(PACK)
        banks = new_banks()
        for g in range(KG):
            sort_w(g, 0)
            for t in every:
                hidden_pass(banks[t], 0, 0, t, g)
        pack_v(nc.scalar.copy, 0, 0, 0, 256)
        pack_v(nc.scalar.copy, 0, 0, 256, 512)
        rows = new_rows()
        relu_out(banks, rows, 0, 0, every)
        banks = new_banks()
        for g in range(KG):
            sort_w(g, 1)
            for t in every:
                hidden_pass(banks[t], 0, 1, t, g)
        pack_v(nc.scalar.copy, 0, 1, 0, 256)
        pack_v(nc.vector.tensor_copy, 1, 0, 0, 512)
        quantize_hidden(rows, 0, 0)
        quantize_v(0, 0)
        rows = new_rows()
        relu_out(banks, rows, 0, 1, every)
        quantize_hidden(rows, 0, 1)
        pack_v(nc.scalar.copy, 0, 1, 256, 512)

        banks = hidden_matmuls(1, 0, every)
        rows_10 = new_rows()
        relu_out(banks, rows_10, 1, 0, every)
        pack_v(nc.vector.tensor_copy, 1, 1, 0, 512)
        quantize_v(1, 0)
        banks = hidden_matmuls(1, 1, every)
        click_0 = click_matmuls(0)
        rows_11 = new_rows()
        relu_out(banks, rows_11, 1, 1, every)
        quantize_v(0, 1)
        quantize_v(1, 1)
        quantize_hidden(rows_10, 1, 0)
        p_click_0 = click_out(0, click_0)
        click_1 = click_matmuls(1)
        p_click_1 = click_out(1, click_1)
        quantize_hidden(rows_11, 1, 1)
        rows_20 = new_rows()
        banks = hidden_matmuls(2, 0, (0, 1))
        conv = conv_matmuls(0)
        relu_out(banks, rows_20, 2, 0, (0, 1))
        conv_out(0, conv, p_click_0)
        banks = hidden_matmuls(2, 0, (2, 3))
        conv = conv_matmuls(1)
        relu_out(banks, rows_20, 2, 0, (2, 3))
        conv_out(1, conv, p_click_1)
        click = click_matmuls(2)
        p_click = click_out(2, click)
        quantize_hidden(rows_20, 2, 0)
        conv = conv_matmuls(2)
        conv_out(2, conv, p_click)
        rows_21 = new_rows()
        for i, ts in ((3, (0, 1)), (4, (2, 3))):
            banks = hidden_matmuls(2, 1, ts)
            click = click_matmuls(i)
            relu_out(banks, rows_21, 2, 1, ts)
            p_click = click_out(i, click)
            if i == 4:
                quantize_hidden(rows_21, 2, 1)
            conv = conv_matmuls(i)
            conv_out(i, conv, p_click)
        for i in range(5, LAST):
            click = click_matmuls(i)
            p_click = click_out(i, click)
            conv = conv_matmuls(i)
            conv_out(i, conv, p_click)
        last_scores(LAST)
